import numpy as np
import ml_dtypes


def mxq(x, axis, fmt="e4m3"):
    dtype, down = {"e4m3": (ml_dtypes.float8_e4m3fn, 7), "e5m2": (ml_dtypes.float8_e5m2, 14)}[fmt]
    v = np.moveaxis(np.asarray(x, np.float32).astype(ml_dtypes.bfloat16).astype(np.float64), axis, -1)
    blocks = v.reshape(v.shape[:-1] + (-1, 32))
    amax = np.abs(blocks).max(-1, keepdims=True)
    byte = np.maximum(np.where(amax > 0, np.frexp(amax)[1] - 1 + 127, 0) - down, 1)
    scale = np.exp2(byte - 127.0)
    codes = (blocks / scale).astype(np.float32).astype(dtype).astype(np.float64)
    return np.moveaxis((codes * scale).reshape(v.shape), -1, axis)


WIDE = False


def mx_kscale(k):
    if not WIDE:
        return np.ones(k)
    levels = np.array([10, -10, 5, -5, 0])
    if k % 512:
        return np.exp2(np.random.permutation(np.resize(levels, k // 32))).repeat(32)
    a = np.empty((k // 512, 16))
    for p in range(k // 512):
        a[p, :8] = np.random.permutation(np.resize(levels, 8))
        for g in range(8):
            far = levels[np.abs(levels - a[p, g]) >= 10]
            a[p, g + 8] = far[np.random.randint(len(far))]
    return np.exp2(a.ravel()).repeat(32)


def f64(x):
    return np.asarray(x).astype(np.float64)


def striped(idx):
    return np.tile(idx.reshape(-1, 16).T, (8, 1)).astype(np.uint16)


def unstriped(offs):
    return offs[:16].T.reshape(-1).astype(np.int64)


def striped8(idx):
    return np.concatenate([x.reshape(-1, 16).T for x in idx]).astype(np.uint16)


def runs(offs, k):
    lists = np.stack([offs[16 * r : 16 * r + 16].T.reshape(-1) for r in range(8)]).astype(np.int64)
    return lists[np.arange(k) % 512 // 64]


def pack_weight(w):
    k, n = w.shape
    w = f64(np.asarray(w, np.float32).astype(ml_dtypes.bfloat16)).reshape(k // 32, 32, n)
    amax = np.abs(w).max(1)
    byte = np.clip(np.where(amax > 0, np.frexp(amax)[1] - 1 + 127 - 7, 1), 1, 254)
    scaled = (w * np.exp2(127.0 - byte)[:, None, :]).reshape(k, n).astype(np.float32)
    words = np.ascontiguousarray(scaled.reshape(k // 512, 128, 4, n).transpose(0, 1, 3, 2)).astype(ml_dtypes.float8_e4m3fn).view(np.uint8)
    return words, np.ascontiguousarray(byte.astype(np.uint8).reshape(k // 512, 16, n))


def unpack_weight(words, scales):
    g, p, n, _ = words.shape
    vals = np.ascontiguousarray(words).view(ml_dtypes.float8_e4m3fn).astype(np.float64) * np.repeat(np.exp2(scales.astype(np.float64) - 127.0), 8, axis=1)[..., None]
    return vals.transpose(0, 1, 3, 2).reshape(g * 512, n)


K, T, S, N, U, H = 512, 2048, 512, 512, 2048, 512


def setup_inputs():
    n = np.random.standard_normal
    s = mx_kscale(K)[:, None]
    u = mx_kscale(H)
    packed_xT = pack_weight(n((K, T)) * s)
    perm = np.stack([np.random.permutation(U) for _ in range(8)])
    return {
        "x_words": packed_xT[0],
        "x_scales": packed_xT[1],
        "w1": (n((K, H)) / np.sqrt(K) / s * u).astype(np.float32),
        "w2": (n((K, H)) / np.sqrt(K) / s * u).astype(np.float32),
        "w3": (n((K, H)) / np.sqrt(K) / s * u).astype(np.float32),
        "w4": (n((K, H)) / np.sqrt(K) / s * u).astype(np.float32),
        "w5": (n((H, N)) / np.sqrt(H) / u[:, None]).astype(np.float32),
        "offs": striped(np.random.permutation(T)[:S]),
        "t2": striped(np.random.permutation(T)[:S]),
        "t3": striped(np.random.permutation(T)[:S]),
        "t4": striped(np.random.permutation(T)[:S]),
        "la": striped8(perm[:, :S]),
        "lb": striped8(perm[:, S:2 * S]),
        "lc": striped8(perm[:, 2 * S:3 * S]),
        "ld": striped8(perm[:, 3 * S:]),
        "mate": striped8(np.stack([np.random.permutation(U) for _ in range(8)])),
    }


def reference(x_words, x_scales, w1, w2, w3, w4, w5, offs, t2, t3, t4, la, lb, lc, ld, mate):
    x_t4 = unpack_weight(x_words, x_scales)[:, unstriped(t4)]
    y4 = mxq(f64(w4), 0, "e4m3").T @ x_t4
    x_t3 = unpack_weight(x_words, x_scales)[:, unstriped(t3)]
    y3 = mxq(f64(w3), 0, "e4m3").T @ x_t3
    x_t2 = unpack_weight(x_words, x_scales)[:, unstriped(t2)]
    y2 = mxq(f64(w2), 0, "e4m3").T @ x_t2
    xq = unpack_weight(x_words, x_scales)[:, unstriped(offs)]
    y1 = mxq(f64(w1), 0, "e4m3").T @ xq
    d0 = np.zeros((H, U))
    d0[np.arange(H)[:, None], runs(la, H)] = y1
    d1 = d0.copy()
    d1[np.arange(H)[:, None], runs(lb, H)] = y2
    d2 = d1.copy()
    d2[np.arange(H)[:, None], runs(lc, H)] = y3
    d3 = d2.copy()
    d3[np.arange(H)[:, None], runs(ld, H)] = y4
    z = d3 - (d3[np.arange(H)[:, None], runs(mate, H)])
    return mxq(f64(w5), 0, "e4m3").T @ mxq(z, 0, "e4m3")

@@ -1,0 +1,187 @@
+from contextlib import ExitStack
+
+import concourse.mybir as mybir
+
+K, T, S, N, U, H = 512, 2048, 512, 512, 2048, 512
+FLOPS = 2 * (4 * K * H * S + H * N * U)
+
+F32 = mybir.dt.float32
+BF16 = mybir.dt.bfloat16
+I32 = mybir.dt.int32
+U32 = mybir.dt.uint32
+U16 = mybir.dt.uint16
+U8 = mybir.dt.uint8
+FP8X4 = mybir.dt.float8_e4m3fn_x4
+COPY = mybir.ActivationFunctionType.Copy
+
+P = 128
+PACK = 4
+CHUNK = 512
+STRIPE = 16
+
+
+def tile_picked_interl4_none_p_kernel(
+    tc, x_words, x_scales, w1, w2, w3, w4, w5, offs, t2, t3, t4, la, lb, lc, ld, mate, out
+):
+    nc = tc.nc
+    with ExitStack() as ctx:
+        keep = ctx.enter_context(tc.tile_pool(name="keep", bufs=1))
+        ring = ctx.enter_context(tc.tile_pool(name="ring", bufs=2))
+        stage = ctx.enter_context(tc.tile_pool(name="stage", bufs=4))
+        psum = ctx.enter_context(tc.psum_pool(name="psum", bufs=4))
+
+        def load_list(name, src):
+            tile = keep.tile(list(src.shape), U16, name=name)
+            nc.sync.dma_start(tile[:], src)
+            return tile
+
+        def load_weight(name, src):
+            raw = keep.tile([P, PACK, src.shape[1]], F32, name=name)
+            nc.sync.dma_start(raw[:], src.rearrange("(p j) c -> p j c", j=PACK))
+            return raw
+
+        def quantize(name, pool, grouped):
+            codes = pool.tile([P, CHUNK], U32, name=name + "_codes", align_bytes=64)
+            scales = pool.tile([P, CHUNK], U8, name=name + "_scales", align_bytes=64)
+            nc.vector.quantize_mx(out=codes[:].bitcast(FP8X4), scales=scales[:], in_=grouped[:])
+            return codes, scales
+
+        def product(acc, lhs, cols, rhs):
+            nc.tensor.matmul_mx(
+                out=acc[:],
+                lhsT=lhs[0][:, cols].bitcast(FP8X4),
+                lhsT_scale=lhs[1][:, cols],
+                rhs=rhs[0][:].bitcast(FP8X4),
+                rhs_scale=rhs[1][:],
+                start=True,
+                stop=True,
+            )
+
+        table_scales = keep.tile([P, T], U8, align_bytes=64)
+        nc.vector.memset(table_scales[:].bitcast(I32), 0)
+        table_words = keep.tile([P, T], I32, align_bytes=64)
+
+        tokens = [load_list("offs", offs)]
+        for q in range(4):
+            nc.sync.dma_start(
+                table_scales[32 * q : 32 * q + 4, :].bitcast(I32),
+                x_scales[0, 4 * q : 4 * q + 4, :].bitcast(I32),
+            )
+        tokens.append(load_list("t2", t2))
+        nc.sync.dma_start(table_words[:], x_words[0].rearrange("p c r -> p (c r)").bitcast(I32))
+        raws = [load_weight("w1", w1)]
+        tokens.append(load_list("t3", t3))
+        places = [load_list("la", la)]
+        raws.append(load_weight("w2", w2))
+        tokens.append(load_list("t4", t4))
+        places.append(load_list("lb", lb))
+        raws.append(load_weight("w3", w3))
+        places.append(load_list("lc", lc))
+        raws.append(load_weight("w4", w4))
+        places.append(load_list("ld", ld))
+        raw5 = load_weight("w5", w5)
+        mates = load_list("mate", mate)
+
+        page = [keep.tile([P, U], F32, name="page%d" % t) for t in range(PACK)]
+
+        for s in range(4):
+            x_bytes = keep.tile([P, S], U8, name="xs%d" % s, align_bytes=64)
+            nc.vector.tensor_copy(x_bytes[:], table_scales[:].indirect(tokens[s][:]))
+            x_codes = keep.tile([P, S], U32, name="xw%d" % s, align_bytes=64)
+            nc.vector.tensor_copy(x_codes[:], table_words[:].bitcast(U32).indirect(tokens[s][:]))
+            grouped = ring.tile([P, PACK * H], BF16, name="w_grouped", align_bytes=64)
+            nc.scalar.copy(
+                out=grouped[:].rearrange("p (t m j) -> p m j t", t=PACK, j=PACK),
+                in_=raws[s][:].rearrange("p j (m t) -> p m j t", t=PACK),
+            )
+            wq = quantize("wq%d" % s, keep, grouped)
+            for t in range(PACK):
+                acc = psum.tile([P, S], F32, name="acc")
+                product(acc, wq, slice(P * t, P * (t + 1)), (x_codes, x_bytes))
+                y = stage.tile([P, S], F32, name="y")
+                nc.scalar.copy(out=y[:], in_=acc[:])
+                nc.vector.tensor_copy(page[t][:].indirect(places[s][:]), y[:])
+
+        grouped = ring.tile([P, PACK * N], BF16, name="w_grouped", align_bytes=64)
+        nc.scalar.copy(
+            out=grouped[:].rearrange("p (c i j) -> p c j i", i=4, j=PACK),
+            in_=raw5[:].rearrange("p j (c i) -> p c j i", i=4),
+        )
+        w5q = quantize("wq5", keep, grouped)
+
+        chunks = U // CHUNK
+        span = PACK + 1
+        work = keep.tile([P, (span * chunks + 1) * CHUNK], F32, align_bytes=64)
+        third = keep.tile([P, U], F32)
+
+        def slot(c, t, count=1):
+            return work[:, (span * c + t) * CHUNK : (span * c + t + count) * CHUNK]
+
+        def own(c, t):
+            if t == 2:
+                return third[:, c * CHUNK : (c + 1) * CHUNK]
+            return slot(c + 1, 0) if t == 3 else slot(c, t + 1)
+
+        for t in range(PACK):
+            for c in range(chunks):
+                nc.scalar.copy(out=own(c, t), in_=page[t][:, c * CHUNK : (c + 1) * CHUNK])
+
+        def project(zq, width, col0, accs, acc0):
+            for b in range(N // P):
+                nc.tensor.matmul_mx(
+                    out=accs[b][:, acc0 : acc0 + width],
+                    lhsT=w5q[0][:, P * b : P * (b + 1)].bitcast(FP8X4),
+                    lhsT_scale=w5q[1][:, P * b : P * (b + 1)],
+                    rhs=zq[0][:].bitcast(FP8X4),
+                    rhs_scale=zq[1][:],
+                    start=True,
+                    stop=True,
+                )
+
+        def quantize_z(z, width, name):
+            codes = ring.tile([P, width], U32, name=name + "_codes", align_bytes=64)
+            scales = ring.tile([P, width], U8, name=name + "_scales", align_bytes=64)
+            nc.vector.quantize_mx(out=codes[:].bitcast(FP8X4), scales=scales[:], in_=z)
+            return codes, scales
+
+        for c in range(U // CHUNK):
+            last = c == U // CHUNK - 1
+            cols = slice(c * CHUNK, (c + 1) * CHUNK)
+            pick = mates[:, c * CHUNK // STRIPE : (c + 1) * CHUNK // STRIPE]
+            for t in range(PACK):
+                nc.vector.tensor_tensor(slot(c, t), page[t][:].indirect(pick), own(c, t), mybir.AluOpType.subtract)
+            minus_z = slot(c, 0, PACK).rearrange("p (t c i) -> p c t i", t=PACK, i=4)
+            accs = [psum.tile([P, CHUNK], F32, name="acc2") for b in range(N // P)]
+            if not last:
+                z = slot(c + 1, 3, 2).bitcast(BF16)
+                nc.scalar.activation(
+                    out=z.rearrange("p (c i t) -> p c t i", i=4, t=PACK), in_=minus_z, func=COPY, scale=-1.0
+                )
+                project(quantize_z(z, CHUNK, "zq"), CHUNK, 0, accs, 0)
+            else:
+                half = CHUNK // 2
+                za = ring.tile([P, PACK * half], BF16, name="zh", align_bytes=64)
+                zb = ring.tile([P, PACK * half], BF16, name="zh", align_bytes=64)
+                nc.vector.tensor_scalar(
+                    out=za[:].rearrange("p (c i t) -> p c t i", i=4, t=PACK),
+                    in0=minus_z[:, : half // 4],
+                    scalar1=-1.0,
+                    scalar2=None,
+                    op0=mybir.AluOpType.mult,
+                )
+                nc.vector.tensor_scalar(
+                    out=zb[:].rearrange("p (c i t) -> p c t i", i=4, t=PACK),
+                    in0=minus_z[:, half // 4 :],
+                    scalar1=-1.0,
+                    scalar2=None,
+                    op0=mybir.AluOpType.mult,
+                )
+                project(quantize_z(za[:], half, "zqh"), half, 0, accs, 0)
+                project(quantize_z(zb[:], half, "zqh"), half, half, accs, half)
+            for b in range(N // P):
+                res = stage.tile([P, CHUNK], F32, name="res")
+                if last and b % 2 == 0:
+                    nc.vector.tensor_copy(out=res[:], in_=accs[b][:])
+                else:
+                    nc.scalar.copy(out=res[:], in_=accs[b][:])
+                nc.sync.dma_start(out[P * b : P * (b + 1), cols], res[:])

@@ -28,7 +28,7 @@ def tile_picked_interl4_none_p_kernel(
         keep = ctx.enter_context(tc.tile_pool(name="keep", bufs=1))
         ring = ctx.enter_context(tc.tile_pool(name="ring", bufs=2))
         stage = ctx.enter_context(tc.tile_pool(name="stage", bufs=4))
-        psum = ctx.enter_context(tc.psum_pool(name="psum", bufs=4))
+        psum = ctx.enter_context(tc.psum_pool(name="psum", bufs=8))
 
         def load_list(name, src):
             tile = keep.tile(list(src.shape), U16, name=name)
@@ -41,14 +41,15 @@ def tile_picked_interl4_none_p_kernel(
             return raw
 
         def quantize(name, pool, grouped):
-            codes = pool.tile([P, CHUNK], U32, name=name + "_codes", align_bytes=64)
-            scales = pool.tile([P, CHUNK], U8, name=name + "_scales", align_bytes=64)
-            nc.vector.quantize_mx(out=codes[:].bitcast(FP8X4), scales=scales[:], in_=grouped[:])
+            width = grouped.shape[1] // PACK
+            codes = pool.tile([P, width], U32, name=name + "_codes", align_bytes=64)
+            scales = pool.tile([P, width], U8, name=name + "_scales", align_bytes=64)
+            nc.vector.quantize_mx(out=codes[:].bitcast(FP8X4), scales=scales[:], in_=grouped)
             return codes, scales
 
         def product(acc, lhs, cols, rhs):
             nc.tensor.matmul_mx(
-                out=acc[:],
+                out=acc,
                 lhsT=lhs[0][:, cols].bitcast(FP8X4),
                 lhsT_scale=lhs[1][:, cols],
                 rhs=rhs[0][:].bitcast(FP8X4),
@@ -61,127 +62,154 @@ def tile_picked_interl4_none_p_kernel(
         nc.vector.memset(table_scales[:].bitcast(I32), 0)
         table_words = keep.tile([P, T], I32, align_bytes=64)
 
+        def load_scales():
+            for q in range(4):
+                nc.sync.dma_start(
+                    table_scales[32 * q : 32 * q + 4, :].bitcast(I32),
+                    x_scales[0, 4 * q : 4 * q + 4, :].bitcast(I32),
+                )
+
+        def load_words():
+            nc.sync.dma_start(table_words[:], x_words[0].rearrange("p c r -> p (c r)").bitcast(I32))
+
         tokens = [load_list("offs", offs)]
-        for q in range(4):
-            nc.sync.dma_start(
-                table_scales[32 * q : 32 * q + 4, :].bitcast(I32),
-                x_scales[0, 4 * q : 4 * q + 4, :].bitcast(I32),
-            )
+        load_scales()
         tokens.append(load_list("t2", t2))
-        nc.sync.dma_start(table_words[:], x_words[0].rearrange("p c r -> p (c r)").bitcast(I32))
+        load_words()
         raws = [load_weight("w1", w1)]
         tokens.append(load_list("t3", t3))
         places = [load_list("la", la)]
         raws.append(load_weight("w2", w2))
         tokens.append(load_list("t4", t4))
-        places.append(load_list("lb", lb))
         raws.append(load_weight("w3", w3))
-        places.append(load_list("lc", lc))
+        places.append(load_list("lb", lb))
         raws.append(load_weight("w4", w4))
+        places.append(load_list("lc", lc))
+        raws.append(load_weight("w5", w5))
         places.append(load_list("ld", ld))
-        raw5 = load_weight("w5", w5)
         mates = load_list("mate", mate)
 
         page = [keep.tile([P, U], F32, name="page%d" % t) for t in range(PACK)]
+        x_codes, x_bytes, wq = {}, {}, {}
 
-        for s in range(4):
-            x_bytes = keep.tile([P, S], U8, name="xs%d" % s, align_bytes=64)
-            nc.vector.tensor_copy(x_bytes[:], table_scales[:].indirect(tokens[s][:]))
-            x_codes = keep.tile([P, S], U32, name="xw%d" % s, align_bytes=64)
-            nc.vector.tensor_copy(x_codes[:], table_words[:].bitcast(U32).indirect(tokens[s][:]))
+        def pick_codes(s):
+            x_codes[s] = keep.tile([P, S], U32, name="xw%d" % s, align_bytes=64)
+            nc.vector.tensor_copy(x_codes[s][:], table_words[:].bitcast(U32).indirect(tokens[s][:]))
+
+        def pick_bytes(s):
+            x_bytes[s] = keep.tile([P, S], U8, name="xs%d" % s, align_bytes=64)
+            nc.vector.tensor_copy(x_bytes[s][:], table_scales[:].indirect(tokens[s][:]))
+
+        def prepare(s):
             grouped = ring.tile([P, PACK * H], BF16, name="w_grouped", align_bytes=64)
-            nc.scalar.copy(
-                out=grouped[:].rearrange("p (t m j) -> p m j t", t=PACK, j=PACK),
-                in_=raws[s][:].rearrange("p j (m t) -> p m j t", t=PACK),
-            )
-            wq = quantize("wq%d" % s, keep, grouped)
-            for t in range(PACK):
-                acc = psum.tile([P, S], F32, name="acc")
-                product(acc, wq, slice(P * t, P * (t + 1)), (x_codes, x_bytes))
-                y = stage.tile([P, S], F32, name="y")
-                nc.scalar.copy(out=y[:], in_=acc[:])
-                nc.vector.tensor_copy(page[t][:].indirect(places[s][:]), y[:])
+            if s < 4:
+                nc.scalar.copy(
+                    out=grouped[:].rearrange("p (t m j) -> p m j t", t=PACK, j=PACK),
+                    in_=raws[s][:].rearrange("p j (m t) -> p m j t", t=PACK),
+                )
+            else:
+                nc.scalar.copy(
+                    out=grouped[:].rearrange("p (c i j) -> p c j i", i=4, j=PACK),
+                    in_=raws[s][:].rearrange("p j (c i) -> p c j i", i=4),
+                )
+            wq[s] = quantize("wq%d" % s, keep, grouped[:])
 
-        grouped = ring.tile([P, PACK * N], BF16, name="w_grouped", align_bytes=64)
-        nc.scalar.copy(
-            out=grouped[:].rearrange("p (c i j) -> p c j i", i=4, j=PACK),
-            in_=raw5[:].rearrange("p j (c i) -> p c j i", i=4),
-        )
-        w5q = quantize("wq5", keep, grouped)
+        def place(s, t):
+            acc = psum.tile([P, S], F32, name="acc")
+            product(acc[:], wq[s], slice(P * t, P * (t + 1)), (x_codes[s], x_bytes[s]))
+            y = stage.tile([P, S], F32, name="y")
+            nc.scalar.copy(out=y[:], in_=acc[:])
+            nc.vector.tensor_copy(page[t][:].indirect(places[s][:]), y[:])
+
+        for s in range(3):
+            pick_bytes(s)
+            pick_codes(s)
+        prepare(0)
+        pick_bytes(3)
+        pick_codes(3)
+        prepare(1)
+        for s in range(4):
+            for t in range(PACK):
+                place(s, t)
+                if t == 1 and s < 3:
+                    prepare(s + 2)
 
         chunks = U // CHUNK
-        span = PACK + 1
-        work = keep.tile([P, (span * chunks + 1) * CHUNK], F32, align_bytes=64)
-        third = keep.tile([P, U], F32)
+        work = keep.tile([P, (PACK * chunks + 2) * CHUNK], F32, align_bytes=64)
+        spare = keep.tile([P, 2, U], F32)
 
         def slot(c, t, count=1):
-            return work[:, (span * c + t) * CHUNK : (span * c + t + count) * CHUNK]
+            return work[:, (PACK * c + t) * CHUNK : (PACK * c + t + count) * CHUNK]
 
         def own(c, t):
-            if t == 2:
-                return third[:, c * CHUNK : (c + 1) * CHUNK]
-            return slot(c + 1, 0) if t == 3 else slot(c, t + 1)
+            if t == 0:
+                return slot(c, 2)
+            if (c, t) == (0, 3):
+                return slot(1, 0, 2)[:, CHUNK // 2 : CHUNK // 2 + CHUNK]
+            if t == 3:
+                return slot(c + 1, 1)
+            return spare[:, t - 1, c * CHUNK : (c + 1) * CHUNK]
 
         for t in range(PACK):
             for c in range(chunks):
                 nc.scalar.copy(out=own(c, t), in_=page[t][:, c * CHUNK : (c + 1) * CHUNK])
 
-        def project(zq, width, col0, accs, acc0):
-            for b in range(N // P):
-                nc.tensor.matmul_mx(
-                    out=accs[b][:, acc0 : acc0 + width],
-                    lhsT=w5q[0][:, P * b : P * (b + 1)].bitcast(FP8X4),
-                    lhsT_scale=w5q[1][:, P * b : P * (b + 1)],
-                    rhs=zq[0][:].bitcast(FP8X4),
-                    rhs_scale=zq[1][:],
-                    start=True,
-                    stop=True,
-                )
-
-        def quantize_z(z, width, name):
-            codes = ring.tile([P, width], U32, name=name + "_codes", align_bytes=64)
-            scales = ring.tile([P, width], U8, name=name + "_scales", align_bytes=64)
-            nc.vector.quantize_mx(out=codes[:].bitcast(FP8X4), scales=scales[:], in_=z)
-            return codes, scales
-
-        for c in range(U // CHUNK):
-            last = c == U // CHUNK - 1
-            cols = slice(c * CHUNK, (c + 1) * CHUNK)
+        def fetch(c):
             pick = mates[:, c * CHUNK // STRIPE : (c + 1) * CHUNK // STRIPE]
             for t in range(PACK):
                 nc.vector.tensor_tensor(slot(c, t), page[t][:].indirect(pick), own(c, t), mybir.AluOpType.subtract)
+
+        def weave(engine, z, c, col0, width):
             minus_z = slot(c, 0, PACK).rearrange("p (t c i) -> p c t i", t=PACK, i=4)
-            accs = [psum.tile([P, CHUNK], F32, name="acc2") for b in range(N // P)]
-            if not last:
-                z = slot(c + 1, 3, 2).bitcast(BF16)
-                nc.scalar.activation(
-                    out=z.rearrange("p (c i t) -> p c t i", i=4, t=PACK), in_=minus_z, func=COPY, scale=-1.0
-                )
-                project(quantize_z(z, CHUNK, "zq"), CHUNK, 0, accs, 0)
+            src = minus_z[:, col0 // 4 : (col0 + width) // 4]
+            dst = z.rearrange("p (c i t) -> p c t i", i=4, t=PACK)
+            if engine == "scalar":
+                nc.scalar.activation(out=dst, in_=src, func=COPY, scale=-1.0)
             else:
-                half = CHUNK // 2
-                za = ring.tile([P, PACK * half], BF16, name="zh", align_bytes=64)
-                zb = ring.tile([P, PACK * half], BF16, name="zh", align_bytes=64)
-                nc.vector.tensor_scalar(
-                    out=za[:].rearrange("p (c i t) -> p c t i", i=4, t=PACK),
-                    in0=minus_z[:, : half // 4],
-                    scalar1=-1.0,
-                    scalar2=None,
-                    op0=mybir.AluOpType.mult,
-                )
-                nc.vector.tensor_scalar(
-                    out=zb[:].rearrange("p (c i t) -> p c t i", i=4, t=PACK),
-                    in0=minus_z[:, half // 4 :],
-                    scalar1=-1.0,
-                    scalar2=None,
-                    op0=mybir.AluOpType.mult,
-                )
-                project(quantize_z(za[:], half, "zqh"), half, 0, accs, 0)
-                project(quantize_z(zb[:], half, "zqh"), half, half, accs, half)
+                nc.vector.tensor_scalar(out=dst, in0=src, scalar1=-1.0, scalar2=None, op0=mybir.AluOpType.mult)
+
+        def drain(engine, acc, dst):
+            res = stage.tile(list(acc.shape), F32, name="res", bufs=8)
+            if engine == "scalar":
+                nc.scalar.copy(out=res[:], in_=acc[:])
+            else:
+                nc.vector.tensor_copy(out=res[:], in_=acc[:])
+            nc.sync.dma_start(dst, res[:])
+
+        half = CHUNK // 2
+        pending = []
+        for c in range(chunks - 1):
+            fetch(c)
+            z = slot(c + 1, 3, 2).bitcast(BF16)
+            weave("scalar", z, c, 0, CHUNK)
+            halves = [z[:, : PACK * half], z[:, PACK * half :]]
+            for acc, dst in pending:
+                drain("scalar", acc, dst)
+            z_codes = ring.tile([P, CHUNK], U32, align_bytes=64)
+            z_scales = ring.tile([P, CHUNK], U8, align_bytes=64)
+            for h in range(2):
+                part = slice(h * half, (h + 1) * half)
+                nc.vector.quantize_mx(out=z_codes[:, part].bitcast(FP8X4), scales=z_scales[:, part], in_=halves[h])
+            pending = []
             for b in range(N // P):
-                res = stage.tile([P, CHUNK], F32, name="res")
-                if last and b % 2 == 0:
-                    nc.vector.tensor_copy(out=res[:], in_=accs[b][:])
-                else:
-                    nc.scalar.copy(out=res[:], in_=accs[b][:])
-                nc.sync.dma_start(out[P * b : P * (b + 1), cols], res[:])
+                acc = psum.tile([P, CHUNK], F32, name="acc")
+                product(acc[:], wq[4], slice(P * b, P * (b + 1)), (z_codes, z_scales))
+                pending.append((acc, out[P * b : P * (b + 1), c * CHUNK : (c + 1) * CHUNK]))
+
+        c = chunks - 1
+        fetch(c)
+        for acc, dst in pending:
+            drain("scalar", acc, dst)
+        out_rows = out.rearrange("(b p) w -> p b w", p=P)
+        pieces = CHUNK // P
+        zs = [stage.tile([P, PACK * P], BF16, name="z_piece", align_bytes=64) for h in range(pieces)]
+        weave("vector", zs[0][:], c, 0, P)
+        for h in range(pieces):
+            if h + 1 < pieces:
+                weave("vector", zs[h + 1][:], c, (h + 1) * P, P)
+            zq = quantize("zq_piece", stage, zs[h][:])
+            acc = psum.tile([P, N // P, P], F32, name="acc")
+            for b in range(N // P):
+                product(acc[:, b, :], wq[4], slice(P * b, P * (b + 1)), zq)
+            col0 = c * CHUNK + h * P
+            drain("vector" if h == pieces - 1 else "scalar", acc, out_rows[:, :, col0 : col0 + P])

from contextlib import ExitStack

import concourse.mybir as mybir

K, T, S, N, U, H = 512, 2048, 512, 512, 2048, 512
FLOPS = 2 * (4 * K * H * S + H * N * U)

F32 = mybir.dt.float32
BF16 = mybir.dt.bfloat16
I32 = mybir.dt.int32
U32 = mybir.dt.uint32
U16 = mybir.dt.uint16
U8 = mybir.dt.uint8
FP8X4 = mybir.dt.float8_e4m3fn_x4
COPY = mybir.ActivationFunctionType.Copy

P = 128
PACK = 4
CHUNK = 512
STRIPE = 16


def tile_picked_interl4_none_p_kernel(
    tc, x_words, x_scales, w1, w2, w3, w4, w5, offs, t2, t3, t4, la, lb, lc, ld, mate, out
):
    nc = tc.nc
    with ExitStack() as ctx:
        keep = ctx.enter_context(tc.tile_pool(name="keep", bufs=1))
        ring = ctx.enter_context(tc.tile_pool(name="ring", bufs=2))
        stage = ctx.enter_context(tc.tile_pool(name="stage", bufs=4))
        psum = ctx.enter_context(tc.psum_pool(name="psum", bufs=8))

        def load_list(name, src):
            tile = keep.tile(list(src.shape), U16, name=name)
            nc.sync.dma_start(tile[:], src)
            return tile

        def load_weight(name, src):
            raw = keep.tile([P, PACK, src.shape[1]], F32, name=name)
            nc.sync.dma_start(raw[:], src.rearrange("(p j) c -> p j c", j=PACK))
            return raw

        def quantize(name, pool, grouped):
            width = grouped.shape[1] // PACK
            codes = pool.tile([P, width], U32, name=name + "_codes", align_bytes=64)
            scales = pool.tile([P, width], U8, name=name + "_scales", align_bytes=64)
            nc.vector.quantize_mx(out=codes[:].bitcast(FP8X4), scales=scales[:], in_=grouped)
            return codes, scales

        def product(acc, lhs, cols, rhs):
            nc.tensor.matmul_mx(
                out=acc,
                lhsT=lhs[0][:, cols].bitcast(FP8X4),
                lhsT_scale=lhs[1][:, cols],
                rhs=rhs[0][:].bitcast(FP8X4),
                rhs_scale=rhs[1][:],
                start=True,
                stop=True,
            )

        table_scales = keep.tile([P, T], U8, align_bytes=64)
        nc.vector.memset(table_scales[:].bitcast(I32), 0)
        table_words = keep.tile([P, T], I32, align_bytes=64)

        def load_scales():
            for q in range(4):
                nc.sync.dma_start(
                    table_scales[32 * q : 32 * q + 4, :].bitcast(I32),
                    x_scales[0, 4 * q : 4 * q + 4, :].bitcast(I32),
                )

        def load_words():
            nc.sync.dma_start(table_words[:], x_words[0].rearrange("p c r -> p (c r)").bitcast(I32))

        tokens = [load_list("offs", offs)]
        load_scales()
        tokens.append(load_list("t2", t2))
        load_words()
        raws = [load_weight("w1", w1)]
        tokens.append(load_list("t3", t3))
        places = [load_list("la", la)]
        raws.append(load_weight("w2", w2))
        tokens.append(load_list("t4", t4))
        raws.append(load_weight("w3", w3))
        places.append(load_list("lb", lb))
        raws.append(load_weight("w4", w4))
        places.append(load_list("lc", lc))
        raws.append(load_weight("w5", w5))
        places.append(load_list("ld", ld))
        mates = load_list("mate", mate)

        page = [keep.tile([P, U], F32, name="page%d" % t) for t in range(PACK)]
        x_codes, x_bytes, wq = {}, {}, {}

        def pick_codes(s):
            x_codes[s] = keep.tile([P, S], U32, name="xw%d" % s, align_bytes=64)
            nc.vector.tensor_copy(x_codes[s][:], table_words[:].bitcast(U32).indirect(tokens[s][:]))

        def pick_bytes(s):
            x_bytes[s] = keep.tile([P, S], U8, name="xs%d" % s, align_bytes=64)
            nc.vector.tensor_copy(x_bytes[s][:], table_scales[:].indirect(tokens[s][:]))

        def prepare(s):
            grouped = ring.tile([P, PACK * H], BF16, name="w_grouped", align_bytes=64)
            if s < 4:
                nc.scalar.copy(
                    out=grouped[:].rearrange("p (t m j) -> p m j t", t=PACK, j=PACK),
                    in_=raws[s][:].rearrange("p j (m t) -> p m j t", t=PACK),
                )
            else:
                nc.scalar.copy(
                    out=grouped[:].rearrange("p (c i j) -> p c j i", i=4, j=PACK),
                    in_=raws[s][:].rearrange("p j (c i) -> p c j i", i=4),
                )
            wq[s] = quantize("wq%d" % s, keep, grouped[:])

        def place(s, t):
            acc = psum.tile([P, S], F32, name="acc")
            product(acc[:], wq[s], slice(P * t, P * (t + 1)), (x_codes[s], x_bytes[s]))
            y = stage.tile([P, S], F32, name="y")
            nc.scalar.copy(out=y[:], in_=acc[:])
            nc.vector.tensor_copy(page[t][:].indirect(places[s][:]), y[:])

        for s in range(3):
            pick_bytes(s)
            pick_codes(s)
        prepare(0)
        pick_bytes(3)
        pick_codes(3)
        prepare(1)
        for s in range(4):
            for t in range(PACK):
                place(s, t)
                if t == 1 and s < 3:
                    prepare(s + 2)

        chunks = U // CHUNK
        work = keep.tile([P, (PACK * chunks + 2) * CHUNK], F32, align_bytes=64)
        spare = keep.tile([P, 2, U], F32)

        def slot(c, t, count=1):
            return work[:, (PACK * c + t) * CHUNK : (PACK * c + t + count) * CHUNK]

        def own(c, t):
            if t == 0:
                return slot(c, 2)
            if (c, t) == (0, 3):
                return slot(1, 0, 2)[:, CHUNK // 2 : CHUNK // 2 + CHUNK]
            if t == 3:
                return slot(c + 1, 1)
            return spare[:, t - 1, c * CHUNK : (c + 1) * CHUNK]

        for t in range(PACK):
            for c in range(chunks):
                nc.scalar.copy(out=own(c, t), in_=page[t][:, c * CHUNK : (c + 1) * CHUNK])

        def fetch(c):
            pick = mates[:, c * CHUNK // STRIPE : (c + 1) * CHUNK // STRIPE]
            for t in range(PACK):
                nc.vector.tensor_tensor(slot(c, t), page[t][:].indirect(pick), own(c, t), mybir.AluOpType.subtract)

        def weave(engine, z, c, col0, width):
            minus_z = slot(c, 0, PACK).rearrange("p (t c i) -> p c t i", t=PACK, i=4)
            src = minus_z[:, col0 // 4 : (col0 + width) // 4]
            dst = z.rearrange("p (c i t) -> p c t i", i=4, t=PACK)
            if engine == "scalar":
                nc.scalar.activation(out=dst, in_=src, func=COPY, scale=-1.0)
            else:
                nc.vector.tensor_scalar(out=dst, in0=src, scalar1=-1.0, scalar2=None, op0=mybir.AluOpType.mult)

        def drain(engine, acc, dst):
            res = stage.tile(list(acc.shape), F32, name="res", bufs=8)
            if engine == "scalar":
                nc.scalar.copy(out=res[:], in_=acc[:])
            else:
                nc.vector.tensor_copy(out=res[:], in_=acc[:])
            nc.sync.dma_start(dst, res[:])

        half = CHUNK // 2
        pending = []
        for c in range(chunks - 1):
            fetch(c)
            z = slot(c + 1, 3, 2).bitcast(BF16)
            weave("scalar", z, c, 0, CHUNK)
            halves = [z[:, : PACK * half], z[:, PACK * half :]]
            for acc, dst in pending:
                drain("scalar", acc, dst)
            z_codes = ring.tile([P, CHUNK], U32, align_bytes=64)
            z_scales = ring.tile([P, CHUNK], U8, align_bytes=64)
            for h in range(2):
                part = slice(h * half, (h + 1) * half)
                nc.vector.quantize_mx(out=z_codes[:, part].bitcast(FP8X4), scales=z_scales[:, part], in_=halves[h])
            pending = []
            for b in range(N // P):
                acc = psum.tile([P, CHUNK], F32, name="acc")
                product(acc[:], wq[4], slice(P * b, P * (b + 1)), (z_codes, z_scales))
                pending.append((acc, out[P * b : P * (b + 1), c * CHUNK : (c + 1) * CHUNK]))

        c = chunks - 1
        fetch(c)
        for acc, dst in pending:
            drain("scalar", acc, dst)
        out_rows = out.rearrange("(b p) w -> p b w", p=P)
        pieces = CHUNK // P
        zs = [stage.tile([P, PACK * P], BF16, name="z_piece", align_bytes=64) for h in range(pieces)]
        weave("vector", zs[0][:], c, 0, P)
        for h in range(pieces):
            if h + 1 < pieces:
                weave("vector", zs[h + 1][:], c, (h + 1) * P, P)
            zq = quantize("zq_piece", stage, zs[h][:])
            acc = psum.tile([P, N // P, P], F32, name="acc")
            for b in range(N // P):
                product(acc[:, b, :], wq[4], slice(P * b, P * (b + 1)), zq)
            col0 = c * CHUNK + h * P
            drain("vector" if h == pieces - 1 else "scalar", acc, out_rows[:, :, col0 : col0 + P])
